import numpy as np, ml_dtypes
CORES = [4,5,6,7,12,13,14,15,20,21,22,23,28,29,30,31]
N = 16
ROOT = 2
WIDTHS = [1,256,0,0,512,51,51,51,0,51,51,51,512,256,512,256]
OFF = [0,1,257,257,257,769,820,871,922,922,973,1024,1075,1587,1843,2355]
C = 2611
def setup_inputs(rng):
    return {"x": rng.standard_normal((N, 128, C), dtype=np.float32).astype(ml_dtypes.bfloat16)}
def reference(x):
    YW = max(WIDTHS)
    y = np.full((N, 128, YW), np.nan, x.dtype)
    for r in range(N):
        y[r][:, :WIDTHS[r]] = x[ROOT][:, OFF[r]:OFF[r] + WIDTHS[r]]
    return {"y": y}

@@ -1,0 +1,40 @@
+SCRATCH = {
+    "stage": ("sbuf", [128, 2611], "bfloat16"),
+    "land": ("sbuf", [128, 512], "bfloat16"),
+}
+SEMAPHORES = ["loaded", "sent", "arrived", "stored"]
+
+
+def rank_program(g, core, T, topo):
+    rank = T.rank_of(core)
+    if rank is None:
+        return
+    widths = T.tables["WIDTHS"]
+    off = T.tables["OFF"]
+    root = T.cores[T.root]
+
+    if core == root:
+        g.sync.dma_start(T.stage[:], T.x[:]).then_inc(T.sem.loaded, 16)
+        g.wait_ge(T.sem.loaded, 16)
+        total = 0
+        for r, dst in enumerate(T.cores):
+            w = widths[r]
+            if w == 0 or dst == core:
+                continue
+            rid, pid, _se = topo.addr(dst)
+            m = topo.mask(core, dst)
+            g.remote_dma(T.land[:, 0:w], T.stage[:, off[r]:off[r] + w], T.sem.arrived, T.sem.sent, pid, rid, m)
+            total += 16 if m == 0xFFFF else 8
+        g.wait_ge(T.sem.sent, total)
+        return
+
+    w = widths[rank]
+    if w == 0:
+        return
+    n = 16 if topo.chip(core) == topo.chip(root) else 8
+    g.wait_ge(T.sem.arrived, n)
+    if w == 1:
+        g.dma_start(T.y[:, 0:1], T.land[:, 0:1], allow_slow_non_contiguous=True).then_inc(T.sem.stored, 16)
+    else:
+        g.dma_start(T.y[:, 0:w], T.land[:, 0:w]).then_inc(T.sem.stored, 16)
+    g.wait_ge(T.sem.stored, 16)

@@ -1,40 +1,99 @@
+from concourse.bass import DstId, RemoteDMATransfer
+
 SCRATCH = {
     "stage": ("sbuf", [128, 2611], "bfloat16"),
+    "hold": ("sbuf", [128, 512], "bfloat16"),
     "land": ("sbuf", [128, 512], "bfloat16"),
 }
-SEMAPHORES = ["loaded", "sent", "arrived", "stored"]
+SEMAPHORES = ["ld0", "ld1", "ld2", "ld3", "handed", "arrived", "sent", "stored", "stored_g"]
+
+LOAD_FROM = [4, 14, 12, 0]
+
+ROOT_CALLS = [
+    (1, [(3, (5, 6, 7), 0x0F00), (1, (9, 10, 11), 0xF000)]),
+    (2, [(18, (14,), 0x000F), (12, (4,), 0x00F0)]),
+    (3, [(2, (12,), 0xFF00)]),
+    (3, [(23, (15,), 0x000F), (29, (13,), 0x00F0)]),
+    (4, [(5, (1,), 0xFF00)]),
+    (4, [(4, (0,), 0xFF00)]),
+]
+OFF_CHIP = 0x00FF
+
+
+def engines(mask):
+    return bin(mask).count("1")
 
 
 def rank_program(g, core, T, topo):
     rank = T.rank_of(core)
-    if rank is None:
-        return
     widths = T.tables["WIDTHS"]
     off = T.tables["OFF"]
     root = T.cores[T.root]
 
+    def is_final(dst, ranks):
+        return len(ranks) == 1 and T.cores[ranks[0]] == dst
+
     if core == root:
-        g.sync.dma_start(T.stage[:], T.x[:]).then_inc(T.sem.loaded, 16)
-        g.wait_ge(T.sem.loaded, 16)
-        total = 0
-        for r, dst in enumerate(T.cores):
-            w = widths[r]
-            if w == 0 or dst == core:
-                continue
-            rid, pid, _se = topo.addr(dst)
-            m = topo.mask(core, dst)
-            g.remote_dma(T.land[:, 0:w], T.stage[:, off[r]:off[r] + w], T.sem.arrived, T.sem.sent, pid, rid, m)
-            total += 16 if m == 0xFFFF else 8
-        g.wait_ge(T.sem.sent, total)
+        starts = sorted(off[r] for r in LOAD_FROM) + [T.tables["C"]]
+        for k, r in enumerate(LOAD_FROM):
+            lo = off[r]
+            hi = starts[starts.index(lo) + 1]
+            q = g.sync if k % 2 == 0 else g.scalar
+            q.dma_start(T.stage[:, lo:hi], T.x[:, lo:hi]).then_inc(T.sem["ld%d" % k], 16)
+        waited = 0
+        left = 0
+        for need, transfers in ROOT_CALLS:
+            while waited < need:
+                g.wait_ge(T.sem["ld%d" % waited], 16)
+                waited += 1
+            call = []
+            for dst, ranks, mask in transfers:
+                lo = off[ranks[0]]
+                hi = off[ranks[-1]] + widths[ranks[-1]]
+                rid, pid, _se = topo.addr(dst)
+                final = is_final(dst, ranks)
+                call.append(RemoteDMATransfer(
+                    dst_ids=[DstId(rid=rid, pnc=pid)],
+                    dma_engine_mask=mask,
+                    remote_sem=T.sem.arrived if final else T.sem.handed,
+                    src=T.stage[:, lo:hi],
+                    dst=(T.land if final else T.hold)[:, 0:hi - lo],
+                ))
+                left += engines(mask)
+            g.remote_dma_fused(call, local_sem=T.sem.sent)
+        g.wait_ge(T.sem.sent, left)
         return
 
-    w = widths[rank]
-    if w == 0:
-        return
-    n = 16 if topo.chip(core) == topo.chip(root) else 8
-    g.wait_ge(T.sem.arrived, n)
-    if w == 1:
-        g.dma_start(T.y[:, 0:1], T.land[:, 0:1], allow_slow_non_contiguous=True).then_inc(T.sem.stored, 16)
-    else:
-        g.dma_start(T.y[:, 0:w], T.land[:, 0:w]).then_inc(T.sem.stored, 16)
-    g.wait_ge(T.sem.stored, 16)
+    job = None
+    arrives = OFF_CHIP
+    for _need, transfers in ROOT_CALLS:
+        for dst, ranks, mask in transfers:
+            if is_final(dst, ranks):
+                if dst == core:
+                    arrives = mask
+            elif dst == core:
+                job = (ranks, mask)
+
+    w = widths[rank] if rank is not None else 0
+
+    if w > 1:
+        g.sync.wait_ge(T.sem.arrived, engines(arrives))
+        g.sync.dma_start(T.y[:, 0:w], T.land[:, 0:w]).then_inc(T.sem.stored, 16)
+
+    if job is not None:
+        ranks, mask = job
+        g.wait_ge(T.sem.handed, engines(mask))
+        base = off[ranks[0]]
+        for r in ranks:
+            rid, pid, _se = topo.addr(T.cores[r])
+            lo = off[r] - base
+            g.remote_dma(T.land[:, 0:widths[r]], T.hold[:, lo:lo + widths[r]],
+                         T.sem.arrived, T.sem.sent, pid, rid, OFF_CHIP)
+        g.wait_ge(T.sem.sent, engines(OFF_CHIP) * len(ranks))
+
+    if w > 1:
+        g.wait_ge(T.sem.stored, 16)
+    elif w == 1:
+        g.wait_ge(T.sem.arrived, engines(arrives))
+        g.dma_start(T.y[:, 0:1], T.land[:, 0:1], allow_slow_non_contiguous=True).then_inc(T.sem.stored_g, 16)
+        g.wait_ge(T.sem.stored_g, 16)

from concourse.bass import DstId, RemoteDMATransfer

SCRATCH = {
    "stage": ("sbuf", [128, 2611], "bfloat16"),
    "hold": ("sbuf", [128, 512], "bfloat16"),
    "land": ("sbuf", [128, 512], "bfloat16"),
}
SEMAPHORES = ["ld0", "ld1", "ld2", "ld3", "handed", "arrived", "sent", "stored", "stored_g"]

LOAD_FROM = [4, 14, 12, 0]

ROOT_CALLS = [
    (1, [(3, (5, 6, 7), 0x0F00), (1, (9, 10, 11), 0xF000)]),
    (2, [(18, (14,), 0x000F), (12, (4,), 0x00F0)]),
    (3, [(2, (12,), 0xFF00)]),
    (3, [(23, (15,), 0x000F), (29, (13,), 0x00F0)]),
    (4, [(5, (1,), 0xFF00)]),
    (4, [(4, (0,), 0xFF00)]),
]
OFF_CHIP = 0x00FF


def engines(mask):
    return bin(mask).count("1")


def rank_program(g, core, T, topo):
    rank = T.rank_of(core)
    widths = T.tables["WIDTHS"]
    off = T.tables["OFF"]
    root = T.cores[T.root]

    def is_final(dst, ranks):
        return len(ranks) == 1 and T.cores[ranks[0]] == dst

    if core == root:
        starts = sorted(off[r] for r in LOAD_FROM) + [T.tables["C"]]
        for k, r in enumerate(LOAD_FROM):
            lo = off[r]
            hi = starts[starts.index(lo) + 1]
            q = g.sync if k % 2 == 0 else g.scalar
            q.dma_start(T.stage[:, lo:hi], T.x[:, lo:hi]).then_inc(T.sem["ld%d" % k], 16)
        waited = 0
        left = 0
        for need, transfers in ROOT_CALLS:
            while waited < need:
                g.wait_ge(T.sem["ld%d" % waited], 16)
                waited += 1
            call = []
            for dst, ranks, mask in transfers:
                lo = off[ranks[0]]
                hi = off[ranks[-1]] + widths[ranks[-1]]
                rid, pid, _se = topo.addr(dst)
                final = is_final(dst, ranks)
                call.append(RemoteDMATransfer(
                    dst_ids=[DstId(rid=rid, pnc=pid)],
                    dma_engine_mask=mask,
                    remote_sem=T.sem.arrived if final else T.sem.handed,
                    src=T.stage[:, lo:hi],
                    dst=(T.land if final else T.hold)[:, 0:hi - lo],
                ))
                left += engines(mask)
            g.remote_dma_fused(call, local_sem=T.sem.sent)
        g.wait_ge(T.sem.sent, left)
        return

    job = None
    arrives = OFF_CHIP
    for _need, transfers in ROOT_CALLS:
        for dst, ranks, mask in transfers:
            if is_final(dst, ranks):
                if dst == core:
                    arrives = mask
            elif dst == core:
                job = (ranks, mask)

    w = widths[rank] if rank is not None else 0

    if w > 1:
        g.sync.wait_ge(T.sem.arrived, engines(arrives))
        g.sync.dma_start(T.y[:, 0:w], T.land[:, 0:w]).then_inc(T.sem.stored, 16)

    if job is not None:
        ranks, mask = job
        g.wait_ge(T.sem.handed, engines(mask))
        base = off[ranks[0]]
        for r in ranks:
            rid, pid, _se = topo.addr(T.cores[r])
            lo = off[r] - base
            g.remote_dma(T.land[:, 0:widths[r]], T.hold[:, lo:lo + widths[r]],
                         T.sem.arrived, T.sem.sent, pid, rid, OFF_CHIP)
        g.wait_ge(T.sem.sent, engines(OFF_CHIP) * len(ranks))

    if w > 1:
        g.wait_ge(T.sem.stored, 16)
    elif w == 1:
        g.wait_ge(T.sem.arrived, engines(arrives))
        g.dma_start(T.y[:, 0:1], T.land[:, 0:1], allow_slow_non_contiguous=True).then_inc(T.sem.stored_g, 16)
        g.wait_ge(T.sem.stored_g, 16)
